import numpy as np
import ml_dtypes

BF16 = ml_dtypes.bfloat16


def bf(x):
    return np.asarray(x, np.float32).astype(BF16)


def f32(x):
    return np.asarray(x, np.float32)


def f64(x):
    return np.asarray(x).astype(np.float64)


def striped(idx):
    return np.concatenate([l.reshape(-1, 16).T for l in idx])


def rows(idx, k):
    return np.tile(np.repeat(idx, 16, axis=0), (k // (16 * 8), 1))


def look(tab, idx):
    return np.take_along_axis(f64(tab), rows(idx, len(tab)), axis=1)


K, S, D, V, N, M = 512, 2048, 4, 512, 2048, 512


def setup_inputs():
    return {"tab": f32(np.random.standard_normal((K, S))), "th": f32(np.random.standard_normal((K, V))), "w": bf(np.random.standard_normal((K, M)) / np.sqrt(K)), "b": f32(0.5 * np.random.standard_normal((M, 1))), "offs": striped(np.stack([np.random.permutation(S)[:N] for _ in range(8)]))}


def reference(tab, th, w, b, offs):
    idx = np.stack([g.T.reshape(-1) for g in np.split(offs, 8)])
    x = sum((look(tab, idx[:, d * V:(d + 1) * V]) >= f64(th)) * 1.0 for d in range(D)) / D
    y = f64(w).T @ x
    return np.maximum(y + f64(b), 0.0)

@@ -1,0 +1,58 @@
+import concourse.mybir as mybir
+
+P = 128
+BF16, F32, U16 = mybir.dt.bfloat16, mybir.dt.float32, mybir.dt.uint16
+K, S, D, V, M = 512, 2048, 4, 512, 512
+FLOPS = 2 * K * M * V
+ROW_BLOCKS = K // P
+OUT_BLOCKS = M // P
+LIST_COLS = V // 16
+
+
+def tile_lookup_vote_ge_relu_kernel(tc, tab, th, w, b, offs, out):
+    nc = tc.nc
+    act = mybir.ActivationFunctionType
+    alu = mybir.AluOpType
+    out_rows = out.rearrange("(p i) j -> p i j", i=OUT_BLOCKS)
+    with (
+        tc.tile_pool(name="held", bufs=1) as held,
+        tc.tile_pool(name="ring", bufs=4) as ring,
+        tc.psum_pool(name="psum", bufs=1) as psum,
+    ):
+        offsets = held.tile([P, D * LIST_COLS], U16, name="offsets")
+        nc.sync.dma_start(offsets[:], offs)
+        windows, thresholds, weights = [], [], []
+        for r in range(ROW_BLOCKS):
+            rows = slice(r * P, (r + 1) * P)
+            window = held.tile([P, S], F32, name=f"window{r}")
+            threshold = held.tile([P, V], F32, name=f"threshold{r}")
+            weight = held.tile([P, P, OUT_BLOCKS], BF16, name=f"weight{r}")
+            nc.sync.dma_start(window[:], tab[rows, :])
+            nc.sync.dma_start(threshold[:], th[rows, :])
+            nc.sync.dma_start(weight[:], w[rows, :].rearrange("k (p i) -> k p i", i=OUT_BLOCKS))
+            windows.append(window)
+            thresholds.append(threshold)
+            weights.append(weight)
+        bias = held.tile([P, OUT_BLOCKS], F32, name="bias")
+        nc.sync.dma_start(bias[:], b.rearrange("(p i) o -> p (i o)", i=OUT_BLOCKS))
+
+        sums = [psum.tile([P, V], F32, name=f"sum{i}") for i in range(OUT_BLOCKS)]
+        for r in range(ROW_BLOCKS):
+            for d in range(D):
+                piece = offsets[:, d * LIST_COLS : (d + 1) * LIST_COLS]
+                vote = ring.tile([P, V], F32, name="vote")
+                nc.vector.tensor_tensor(vote[:], windows[r][:].indirect(piece), thresholds[r][:], alu.is_ge)
+                share = ring.tile([P, V], BF16, name="share")
+                nc.scalar.activation(share[:], vote[:], act.Copy, scale=1.0 / D)
+                first = r == 0 and d == 0
+                last = r == ROW_BLOCKS - 1 and d == D - 1
+                for i in range(OUT_BLOCKS):
+                    nc.tensor.matmul(sums[i][:], weights[r][:, :, i], share[:], start=first, stop=last)
+
+        for i in range(OUT_BLOCKS):
+            result = held.tile([P, V], F32, name=f"result{i}")
+            if i % 2 == 0:
+                nc.scalar.activation(result[:], sums[i][:], act.Relu, bias=bias[:, i : i + 1])
+            else:
+                nc.vector.tensor_scalar(result[:], sums[i][:], bias[:, i : i + 1], 0.0, alu.add, alu.max)
+            nc.sync.dma_start(out_rows[:, i, :], result[:])

@@ -7,6 +7,7 @@ FLOPS = 2 * K * M * V
 ROW_BLOCKS = K // P
 OUT_BLOCKS = M // P
 LIST_COLS = V // 16
+WARM_UPS = 14
 
 
 def tile_lookup_vote_ge_relu_kernel(tc, tab, th, w, b, offs, out):
@@ -26,15 +27,25 @@ def tile_lookup_vote_ge_relu_kernel(tc, tab, th, w, b, offs, out):
             rows = slice(r * P, (r + 1) * P)
             window = held.tile([P, S], F32, name=f"window{r}")
             threshold = held.tile([P, V], F32, name=f"threshold{r}")
-            weight = held.tile([P, P, OUT_BLOCKS], BF16, name=f"weight{r}")
+            loaded = held.tile([P, M], BF16, name=f"loaded{r}")
             nc.sync.dma_start(window[:], tab[rows, :])
             nc.sync.dma_start(threshold[:], th[rows, :])
-            nc.sync.dma_start(weight[:], w[rows, :].rearrange("k (p i) -> k p i", i=OUT_BLOCKS))
+            nc.sync.dma_start(loaded[:], w[rows, :])
+            weight = held.tile([P, OUT_BLOCKS, P], BF16, name=f"weight{r}")
+            nc.scalar.activation(
+                weight[:], loaded[:].rearrange("k (p i) -> k i p", i=OUT_BLOCKS), act.Copy, scale=1.0 / D
+            )
             windows.append(window)
             thresholds.append(threshold)
             weights.append(weight)
         bias = held.tile([P, OUT_BLOCKS], F32, name="bias")
         nc.sync.dma_start(bias[:], b.rearrange("(p i) o -> p (i o)", i=OUT_BLOCKS))
+
+        zeros = held.tile([P, V], BF16, name="zeros")
+        nc.gpsimd.memset(zeros[:], 0.0)
+        idle = psum.tile([P, V], F32, name="idle")
+        for n in range(WARM_UPS):
+            nc.tensor.matmul(idle[:], zeros[:, :P], zeros[:], start=True, stop=True)
 
         sums = [psum.tile([P, V], F32, name=f"sum{i}") for i in range(OUT_BLOCKS)]
         for r in range(ROW_BLOCKS):
@@ -42,12 +53,11 @@ def tile_lookup_vote_ge_relu_kernel(tc, tab, th, w, b, offs, out):
                 piece = offsets[:, d * LIST_COLS : (d + 1) * LIST_COLS]
                 vote = ring.tile([P, V], F32, name="vote")
                 nc.vector.tensor_tensor(vote[:], windows[r][:].indirect(piece), thresholds[r][:], alu.is_ge)
-                share = ring.tile([P, V], BF16, name="share")
-                nc.scalar.activation(share[:], vote[:], act.Copy, scale=1.0 / D)
+                vote_bf16 = vote[:].bitcast(BF16)[:, 1::2]
                 first = r == 0 and d == 0
                 last = r == ROW_BLOCKS - 1 and d == D - 1
                 for i in range(OUT_BLOCKS):
-                    nc.tensor.matmul(sums[i][:], weights[r][:, :, i], share[:], start=first, stop=last)
+                    nc.tensor.matmul(sums[i][:], weights[r][:, i, :], vote_bf16, start=first, stop=last)
 
         for i in range(OUT_BLOCKS):
             result = held.tile([P, V], F32, name=f"result{i}")

@@ -7,7 +7,14 @@ FLOPS = 2 * K * M * V
 ROW_BLOCKS = K // P
 OUT_BLOCKS = M // P
 LIST_COLS = V // 16
+PSUM_BANKS = 8
+PARTS = PSUM_BANKS // OUT_BLOCKS
+PART = V // PARTS
 WARM_UPS = 14
+
+
+def upper_halves(tile):
+    return tile[:].bitcast(BF16)[:, 1::2]
 
 
 def tile_lookup_vote_ge_relu_kernel(tc, tab, th, w, b, offs, out):
@@ -21,48 +28,49 @@ def tile_lookup_vote_ge_relu_kernel(tc, tab, th, w, b, offs, out):
         tc.psum_pool(name="psum", bufs=1) as psum,
     ):
         offsets = held.tile([P, D * LIST_COLS], U16, name="offsets")
-        nc.sync.dma_start(offsets[:], offs)
         windows, thresholds, weights = [], [], []
         for r in range(ROW_BLOCKS):
             rows = slice(r * P, (r + 1) * P)
-            window = held.tile([P, S], F32, name=f"window{r}")
             threshold = held.tile([P, V], F32, name=f"threshold{r}")
-            loaded = held.tile([P, M], BF16, name=f"loaded{r}")
-            nc.sync.dma_start(window[:], tab[rows, :])
+            window = held.tile([P, S], F32, name=f"window{r}")
+            loaded = held.tile([P, P, OUT_BLOCKS], BF16, name=f"loaded{r}")
             nc.sync.dma_start(threshold[:], th[rows, :])
-            nc.sync.dma_start(loaded[:], w[rows, :])
+            nc.sync.dma_start(window[:], tab[rows, :])
+            if r == 0:
+                nc.sync.dma_start(offsets[:], offs)
+            nc.sync.dma_start(loaded[:], w[rows, :].rearrange("k (p i) -> k p i", i=OUT_BLOCKS))
             weight = held.tile([P, OUT_BLOCKS, P], BF16, name=f"weight{r}")
-            nc.scalar.activation(
-                weight[:], loaded[:].rearrange("k (p i) -> k i p", i=OUT_BLOCKS), act.Copy, scale=1.0 / D
-            )
+            for i in range(OUT_BLOCKS):
+                nc.scalar.activation(weight[:, i, :], loaded[:, :, i], act.Copy, scale=1.0 / D)
             windows.append(window)
             thresholds.append(threshold)
             weights.append(weight)
         bias = held.tile([P, OUT_BLOCKS], F32, name="bias")
         nc.sync.dma_start(bias[:], b.rearrange("(p i) o -> p (i o)", i=OUT_BLOCKS))
 
-        zeros = held.tile([P, V], BF16, name="zeros")
-        nc.gpsimd.memset(zeros[:], 0.0)
-        idle = psum.tile([P, V], F32, name="idle")
-        for n in range(WARM_UPS):
-            nc.tensor.matmul(idle[:], zeros[:, :P], zeros[:], start=True, stop=True)
+        pieces = [(i, slice(c * PART, (c + 1) * PART)) for i in range(OUT_BLOCKS) for c in range(PARTS)]
+        sums = [psum.tile([P, PART], F32, name=f"sum{n}") for n in range(len(pieces))]
 
-        sums = [psum.tile([P, V], F32, name=f"sum{i}") for i in range(OUT_BLOCKS)]
+        zeros = held.tile([P, P], BF16, name="zeros")
+        nc.gpsimd.memset(zeros[:], 0.0)
+        for n in range(WARM_UPS):
+            nc.tensor.matmul(sums[0][:], zeros[:], upper_halves(thresholds[0])[:, :PART], start=True, stop=True)
+
         for r in range(ROW_BLOCKS):
             for d in range(D):
-                piece = offsets[:, d * LIST_COLS : (d + 1) * LIST_COLS]
+                entries = offsets[:, d * LIST_COLS : (d + 1) * LIST_COLS]
                 vote = ring.tile([P, V], F32, name="vote")
-                nc.vector.tensor_tensor(vote[:], windows[r][:].indirect(piece), thresholds[r][:], alu.is_ge)
-                vote_bf16 = vote[:].bitcast(BF16)[:, 1::2]
+                nc.vector.tensor_tensor(vote[:], windows[r][:].indirect(entries), thresholds[r][:], alu.is_ge)
+                vote_bf16 = upper_halves(vote)
                 first = r == 0 and d == 0
                 last = r == ROW_BLOCKS - 1 and d == D - 1
-                for i in range(OUT_BLOCKS):
-                    nc.tensor.matmul(sums[i][:], weights[r][:, i, :], vote_bf16, start=first, stop=last)
+                for n, (i, cols) in enumerate(pieces):
+                    nc.tensor.matmul(sums[n][:], weights[r][:, i, :], vote_bf16[:, cols], start=first, stop=last)
 
-        for i in range(OUT_BLOCKS):
-            result = held.tile([P, V], F32, name=f"result{i}")
-            if i % 2 == 0:
-                nc.scalar.activation(result[:], sums[i][:], act.Relu, bias=bias[:, i : i + 1])
+        for n, (i, cols) in enumerate(pieces):
+            result = held.tile([P, PART], F32, name=f"result{n}")
+            if n % 2 == 0:
+                nc.scalar.activation(result[:], sums[n][:], act.Relu, bias=bias[:, i : i + 1])
             else:
-                nc.vector.tensor_scalar(result[:], sums[i][:], bias[:, i : i + 1], 0.0, alu.add, alu.max)
-            nc.sync.dma_start(out_rows[:, i, :], result[:])
+                nc.vector.tensor_scalar(result[:], sums[n][:], bias[:, i : i + 1], 0.0, alu.add, alu.max)
+            nc.sync.dma_start(out_rows[:, i, cols], result[:])

@@ -24,7 +24,6 @@ def tile_lookup_vote_ge_relu_kernel(tc, tab, th, w, b, offs, out):
     out_rows = out.rearrange("(p i) j -> p i j", i=OUT_BLOCKS)
     with (
         tc.tile_pool(name="held", bufs=1) as held,
-        tc.tile_pool(name="ring", bufs=4) as ring,
         tc.psum_pool(name="psum", bufs=1) as psum,
     ):
         offsets = held.tile([P, D * LIST_COLS], U16, name="offsets")
@@ -59,7 +58,7 @@ def tile_lookup_vote_ge_relu_kernel(tc, tab, th, w, b, offs, out):
         for r in range(ROW_BLOCKS):
             for d in range(D):
                 entries = offsets[:, d * LIST_COLS : (d + 1) * LIST_COLS]
-                vote = ring.tile([P, V], F32, name="vote")
+                vote = held.tile([P, V], F32, name=f"vote{r}_{d}")
                 nc.vector.tensor_tensor(vote[:], windows[r][:].indirect(entries), thresholds[r][:], alu.is_ge)
                 vote_bf16 = upper_halves(vote)
                 first = r == 0 and d == 0

@@ -10,7 +10,6 @@ LIST_COLS = V // 16
 PSUM_BANKS = 8
 PARTS = PSUM_BANKS // OUT_BLOCKS
 PART = V // PARTS
-WARM_UPS = 14
 
 
 def upper_halves(tile):
@@ -49,11 +48,6 @@ def tile_lookup_vote_ge_relu_kernel(tc, tab, th, w, b, offs, out):
 
         pieces = [(i, slice(c * PART, (c + 1) * PART)) for i in range(OUT_BLOCKS) for c in range(PARTS)]
         sums = [psum.tile([P, PART], F32, name=f"sum{n}") for n in range(len(pieces))]
-
-        zeros = held.tile([P, P], BF16, name="zeros")
-        nc.gpsimd.memset(zeros[:], 0.0)
-        for n in range(WARM_UPS):
-            nc.tensor.matmul(sums[0][:], zeros[:], upper_halves(thresholds[0])[:, :PART], start=True, stop=True)
 
         for r in range(ROW_BLOCKS):
             for d in range(D):

import concourse.mybir as mybir

P = 128
BF16, F32, U16 = mybir.dt.bfloat16, mybir.dt.float32, mybir.dt.uint16
K, S, D, V, M = 512, 2048, 4, 512, 512
FLOPS = 2 * K * M * V
ROW_BLOCKS = K // P
OUT_BLOCKS = M // P
LIST_COLS = V // 16
PSUM_BANKS = 8
PARTS = PSUM_BANKS // OUT_BLOCKS
PART = V // PARTS


def upper_halves(tile):
    return tile[:].bitcast(BF16)[:, 1::2]


def tile_lookup_vote_ge_relu_kernel(tc, tab, th, w, b, offs, out):
    nc = tc.nc
    act = mybir.ActivationFunctionType
    alu = mybir.AluOpType
    out_rows = out.rearrange("(p i) j -> p i j", i=OUT_BLOCKS)
    with (
        tc.tile_pool(name="held", bufs=1) as held,
        tc.psum_pool(name="psum", bufs=1) as psum,
    ):
        offsets = held.tile([P, D * LIST_COLS], U16, name="offsets")
        windows, thresholds, weights = [], [], []
        for r in range(ROW_BLOCKS):
            rows = slice(r * P, (r + 1) * P)
            threshold = held.tile([P, V], F32, name=f"threshold{r}")
            window = held.tile([P, S], F32, name=f"window{r}")
            loaded = held.tile([P, P, OUT_BLOCKS], BF16, name=f"loaded{r}")
            nc.sync.dma_start(threshold[:], th[rows, :])
            nc.sync.dma_start(window[:], tab[rows, :])
            if r == 0:
                nc.sync.dma_start(offsets[:], offs)
            nc.sync.dma_start(loaded[:], w[rows, :].rearrange("k (p i) -> k p i", i=OUT_BLOCKS))
            weight = held.tile([P, OUT_BLOCKS, P], BF16, name=f"weight{r}")
            for i in range(OUT_BLOCKS):
                nc.scalar.activation(weight[:, i, :], loaded[:, :, i], act.Copy, scale=1.0 / D)
            windows.append(window)
            thresholds.append(threshold)
            weights.append(weight)
        bias = held.tile([P, OUT_BLOCKS], F32, name="bias")
        nc.sync.dma_start(bias[:], b.rearrange("(p i) o -> p (i o)", i=OUT_BLOCKS))

        pieces = [(i, slice(c * PART, (c + 1) * PART)) for i in range(OUT_BLOCKS) for c in range(PARTS)]
        sums = [psum.tile([P, PART], F32, name=f"sum{n}") for n in range(len(pieces))]

        for r in range(ROW_BLOCKS):
            for d in range(D):
                entries = offsets[:, d * LIST_COLS : (d + 1) * LIST_COLS]
                vote = held.tile([P, V], F32, name=f"vote{r}_{d}")
                nc.vector.tensor_tensor(vote[:], windows[r][:].indirect(entries), thresholds[r][:], alu.is_ge)
                vote_bf16 = upper_halves(vote)
                first = r == 0 and d == 0
                last = r == ROW_BLOCKS - 1 and d == D - 1
                for n, (i, cols) in enumerate(pieces):
                    nc.tensor.matmul(sums[n][:], weights[r][:, i, :], vote_bf16[:, cols], start=first, stop=last)

        for n, (i, cols) in enumerate(pieces):
            result = held.tile([P, PART], F32, name=f"result{n}")
            if n % 2 == 0:
                nc.scalar.activation(result[:], sums[n][:], act.Relu, bias=bias[:, i : i + 1])
            else:
                nc.vector.tensor_scalar(result[:], sums[n][:], bias[:, i : i + 1], 0.0, alu.add, alu.max)
            nc.sync.dma_start(out_rows[:, i, cols], result[:])
